import numpy as np
import ml_dtypes


def mxq(x, axis, fmt="e4m3"):
    dtype, down = {"e4m3": (ml_dtypes.float8_e4m3fn, 7), "e5m2": (ml_dtypes.float8_e5m2, 14)}[fmt]
    v = np.moveaxis(np.asarray(x, np.float32).astype(ml_dtypes.bfloat16).astype(np.float64), axis, -1)
    blocks = v.reshape(v.shape[:-1] + (-1, 32))
    amax = np.abs(blocks).max(-1, keepdims=True)
    byte = np.maximum(np.where(amax > 0, np.frexp(amax)[1] - 1 + 127, 0) - down, 1)
    scale = np.exp2(byte - 127.0)
    codes = (blocks / scale).astype(np.float32).astype(dtype).astype(np.float64)
    return np.moveaxis((codes * scale).reshape(v.shape), -1, axis)


WIDE = False


def mx_kscale(k):
    if not WIDE:
        return np.ones(k)
    levels = np.array([10, -10, 5, -5, 0])
    if k % 512:
        return np.exp2(np.random.permutation(np.resize(levels, k // 32))).repeat(32)
    a = np.empty((k // 512, 16))
    for p in range(k // 512):
        a[p, :8] = np.random.permutation(np.resize(levels, 8))
        for g in range(8):
            far = levels[np.abs(levels - a[p, g]) >= 10]
            a[p, g + 8] = far[np.random.randint(len(far))]
    return np.exp2(a.ravel()).repeat(32)


def f64(x):
    return np.asarray(x).astype(np.float64)


def striped(idx):
    return np.tile(np.asarray(idx).reshape(-1, 16).T, (8, 1)).astype(np.uint16)


def unstriped(offs):
    return offs[:16].T.reshape(-1).astype(np.int64)


E2M1 = np.array([0.0, 0.5, 1.0, 1.5, 2.0, 3.0, 4.0, 6.0, -0.0, -0.5, -1.0, -1.5, -2.0, -3.0, -4.0, -6.0])


def pack_weight(w, fmt):
    k, n = w.shape
    w = f64(np.asarray(w, np.float32).astype(ml_dtypes.bfloat16)).reshape(k // 32, 32, n)
    amax = np.abs(w).max(1)
    if fmt == "e4m3":
        byte = np.frexp(amax)[1] - 1 + 127 - 7
    else:
        mant, ex = np.frexp(amax / 6.0)
        byte = np.where(mant > 0.5, ex, ex - 1) + 127
    byte = np.clip(np.where(amax > 0, byte, 1), 1, 254)
    scaled = (w * np.exp2(127.0 - byte)[:, None, :]).reshape(k, n).astype(np.float32)
    by_word = np.ascontiguousarray(scaled.reshape(k // 512, 128, 4, n).transpose(0, 1, 3, 2))
    if fmt == "e4m3":
        words = by_word.astype(ml_dtypes.float8_e4m3fn).view(np.uint8)
    else:
        c = by_word.astype(ml_dtypes.float4_e2m1fn).view(np.uint8) & 0xF
        words = (c[..., 0::2] | (c[..., 1::2] << 4)).reshape(k // 512, 128, 2 * n)
    return np.ascontiguousarray(words), np.ascontiguousarray(byte.astype(np.uint8).reshape(k // 512, 16, n))


def unpack_weight(words, scales, fmt):
    g, _, n = scales.shape
    words = np.ascontiguousarray(words).reshape(g, 128, n, -1)
    if fmt == "e4m3":
        vals = words.view(ml_dtypes.float8_e4m3fn).astype(np.float64)
    else:
        nib = np.empty((g, 128, n, 4), np.uint8)
        nib[..., 0::2] = words & 0xF
        nib[..., 1::2] = words >> 4
        vals = E2M1[nib]
    vals = vals * np.repeat(np.exp2(scales.astype(np.float64) - 127.0), 8, axis=1)[..., None]
    return vals.transpose(0, 1, 3, 2).reshape(g * 512, n)


def sigmoid(v):
    return 1.0 / (1.0 + np.exp(-v))


D, E, T, I, Q, G = 512, 512, 2048, 512, 128, 32


def setup_inputs():
    n = np.random.standard_normal
    idx = np.random.permutation(T)[:I]
    fd = mx_kscale(D)
    fe = mx_kscale(E)
    keysp = pack_weight(n((D, T)) / fd[:, None], "e2m1")
    valsp = pack_weight(n((E, T)) / fe[:, None], "e2m1")
    return {
        "query": (n((D, Q)) * 0.5 / np.sqrt(D) * fd[:, None]).astype(np.float32),
        "keys_words": keysp[0],
        "keys_scales": keysp[1],
        "helpf": (np.random.uniform(0.5, 1.5, (Q, 1))).astype(np.float32),
        "gout": (n((E, Q)) * 1 / np.sqrt(E) * fe[:, None]).astype(np.float32),
        "vals_words": valsp[0],
        "vals_scales": valsp[1],
        "old": (0.5 * n((Q, T))).astype(np.float32),
        "offs": striped(idx),
    }


def reference(query, keys_words, keys_scales, helpf, gout, vals_words, vals_scales, old, offs):
    idx = unstriped(offs)
    keysu = unpack_weight(keys_words, keys_scales, "e2m1")
    valsu = unpack_weight(vals_words, vals_scales, "e2m1")
    queryq = mxq(f64(query), 0, "e4m3")
    keysidxg = keysu[:, idx]
    a = queryq.T @ keysidxg
    m1 = a.reshape(Q, G, I // G).mean(axis=2)
    gt = sigmoid(m1 * 4.0)
    gr = np.repeat(gt, I // G, axis=1)
    s = a * (gr * f64(helpf) + 1.0)
    p = np.exp(s - np.max(s, axis=1, keepdims=True))
    z = np.sum(p, axis=1, keepdims=True)
    goutq = mxq(f64(gout), 0, "e4m3")
    valsidxg = valsu[:, idx]
    c0 = goutq.T @ valsidxg
    dz = np.sum(c0 * p / np.square(z) * (-1.0), axis=1, keepdims=True)
    dp = c0 / z + dz
    ds = dp * p
    dgr = ds * a * f64(helpf)
    dgt = dgr.reshape(Q, G, I // G).sum(axis=2)
    dm1 = dgt * gt * (1.0 - gt) * 4.0
    e1 = dm1 / 16.0
    r1 = np.repeat(e1, I // G, axis=1)
    da = ds * (gr * f64(helpf) + 1.0) + r1
    gs = da * 512.0
    gf = np.zeros((Q, T))
    gf[:, idx] = gs
    y = f64(old) + gf
    return y

@@ -1,0 +1,200 @@
+from contextlib import ExitStack
+
+import concourse.mybir as mybir
+
+F32 = mybir.dt.float32
+BF16 = mybir.dt.bfloat16
+I32 = mybir.dt.int32
+U32 = mybir.dt.uint32
+U16 = mybir.dt.uint16
+U8 = mybir.dt.uint8
+FP8X4 = mybir.dt.float8_e4m3fn_x4
+FP4X4 = mybir.dt.float4_e2m1fn_x4
+ALU = mybir.AluOpType
+ACT = mybir.ActivationFunctionType
+AX = mybir.AxisListType
+
+P = 128
+D = 512
+T = 2048
+SLOTS = 512
+PAGE = 16
+PAGES = SLOTS // PAGE
+HALF = SLOTS // 2
+HPAGES = PAGES // 2
+OUT_CHUNKS = (256, 512, 512, 512, 256)
+
+FLOPS = 2 * 2 * D * P * SLOTS
+
+
+def tile_attend_bpagemates_s_kernel(tc, query, keys_words, keys_scales, helpf, gout, vals_words, vals_scales, old, offs, out):
+    nc = tc.nc
+    with ExitStack() as ctx:
+        sb = ctx.enter_context(tc.tile_pool(name="sb", bufs=1))
+        ps = ctx.enter_context(tc.psum_pool(name="ps", bufs=1))
+
+        def by_page(ap):
+            return ap.rearrange("p (g j) -> p g j", j=PAGE)
+
+        def over_page(ap, n):
+            return ap.unsqueeze(2).to_broadcast([P, n, PAGE])
+
+        offsets = sb.tile([P, SLOTS // 16], U16, name="offsets")
+        k_words = sb.tile([P, T], U16, name="k_words")
+        v_words = sb.tile([P, T], U16, name="v_words")
+        k_bytes = sb.tile([P, T], U8, name="k_bytes")
+        v_bytes = sb.tile([P, T], U8, name="v_bytes")
+        q_raw = sb.tile([P, 4, P], F32, name="q_raw")
+        g_raw = sb.tile([P, 4, P], F32, name="g_raw")
+        help_col = sb.tile([P, 1], F32, name="help_col")
+        result = sb.tile([P, T], F32, name="result")
+        window = sb.tile([P, T], F32, name="window")
+
+        nc.vector.memset(k_bytes[:].bitcast(I32), 0)
+        nc.vector.memset(v_bytes[:].bitcast(I32), 0)
+        nc.vector.memset(window[:], 0.0)
+
+        def load_scale_rows(engine, tile, src):
+            for quad in range(4):
+                engine.dma_start(
+                    out=tile[32 * quad : 32 * quad + 4, :].bitcast(I32),
+                    in_=src[0, 4 * quad : 4 * quad + 4, :].bitcast(I32),
+                )
+
+        nc.sync.dma_start(offsets[:], offs)
+        nc.sync.dma_start(out=k_words[:].bitcast(I32), in_=keys_words[0].bitcast(I32))
+        load_scale_rows(nc.scalar, k_bytes, keys_scales)
+        nc.sync.dma_start(out=q_raw[:], in_=query.rearrange("(p j) w -> p j w", j=4))
+        nc.sync.dma_start(out=v_words[:].bitcast(I32), in_=vals_words[0].bitcast(I32))
+        nc.sync.dma_start(out=help_col[:], in_=helpf)
+        nc.sync.dma_start(out=g_raw[:], in_=gout.rearrange("(p j) w -> p j w", j=4))
+        load_scale_rows(nc.sync, v_bytes, vals_scales)
+        nc.sync.dma_start(out=result[:], in_=old)
+
+        def round_and_interleave(raw, name):
+            grouped = sb.tile([P, P, 4], BF16, name=name, align_bytes=64)
+            nc.scalar.activation(out=grouped[:], in_=raw[:].rearrange("p j w -> p w j"), func=ACT.Copy)
+            return grouped
+
+        def quantise(grouped, name):
+            codes = sb.tile([P, P], U32, name=name + "_codes", align_bytes=64)
+            scales = sb.tile([P, P], U8, name=name + "_scales", align_bytes=64)
+            nc.vector.quantize_mx(out=codes[:].bitcast(FP8X4), scales=scales[:], in_=grouped[:].rearrange("p w j -> p (w j)"))
+            return codes, scales
+
+        q_bf = round_and_interleave(q_raw, "q_bf")
+        consts = sb.tile([P, 4], F32, name="consts")
+        nc.scalar.activation(out=consts[:, 0:1], in_=help_col[:], func=ACT.Identity, scale=0.5, bias=1.0)
+        nc.scalar.activation(out=consts[:, 1:2], in_=help_col[:], func=ACT.Copy, scale=0.5)
+        nc.scalar.activation(out=consts[:, 2:3], in_=help_col[:], func=ACT.Copy, scale=32.0)
+        nc.scalar.activation(out=consts[:, 3:4], in_=help_col[:], func=ACT.Copy, scale=-32.0)
+        g_bf = round_and_interleave(g_raw, "g_bf")
+
+        halves = [slice(h * HALF, (h + 1) * HALF) for h in range(2)]
+        page_halves = [slice(h * HPAGES, (h + 1) * HPAGES) for h in range(2)]
+        list_halves = [offsets[:, h * HALF // 16 : (h + 1) * HALF // 16] for h in range(2)]
+
+        a = []
+        for h in range(2):
+            ks = sb.tile([P, HALF], U8, name="ks%d" % h, tag="ks_then_vw%d" % h, align_bytes=64)
+            nc.vector.tensor_copy(ks[:], k_bytes[:].indirect(list_halves[h]))
+            kw = sb.tile([P, HALF], U16, name="kw%d" % h, align_bytes=64)
+            nc.vector.tensor_copy(kw[:], k_words[:].indirect(list_halves[h]))
+            if h == 0:
+                q_codes, q_scales = quantise(q_bf, "q")
+            bank = ps.tile([P, HALF], F32, name="a%d" % h)
+            nc.tensor.matmul_mx(
+                out=bank[:], lhsT=q_codes[:].bitcast(FP8X4), lhsT_scale=q_scales[:],
+                rhs=kw[:].bitcast(FP4X4), rhs_scale=ks[:], start=True, stop=True,
+            )
+            a.append(bank)
+
+        page_sum = sb.tile([P, PAGES], F32, name="page_sum")
+        th = sb.tile([P, PAGES], F32, name="th")
+        boost = sb.tile([P, PAGES], F32, name="boost", tag="boost_then_vs", align_bytes=64)
+        for h in range(2):
+            nc.vector.tensor_reduce(out=page_sum[:, page_halves[h]], in_=by_page(a[h][:]), axis=AX.X, op=ALU.add)
+        for pages in page_halves:
+            nc.scalar.activation(out=th[:, pages], in_=page_sum[:, pages], func=ACT.Tanh, scale=0.125)
+        for pages in page_halves:
+            nc.scalar.activation(out=boost[:, pages], in_=th[:, pages], func=ACT.Identity, scale=consts[:, 1:2], bias=consts[:, 0:1])
+
+        vw = []
+        for h in range(2):
+            words = sb.tile([P, HALF], U16, name="vw%d" % h, tag="ks_then_vw%d" % h, align_bytes=64)
+            nc.vector.tensor_copy(words[:], v_words[:].indirect(list_halves[h]))
+            vw.append(words)
+        g_codes, g_scales = quantise(g_bf, "g")
+
+        s = sb.tile([P, SLOTS], F32, name="s")
+        for h in range(2):
+            nc.vector.tensor_tensor(
+                out=by_page(s[:, halves[h]]), in0=by_page(a[h][:]), in1=over_page(boost[:, page_halves[h]], HPAGES), op=ALU.mult
+            )
+        neg_max = sb.tile([P, 1], F32, name="neg_max")
+        nc.vector.tensor_reduce(out=neg_max[:], in_=s[:], axis=AX.X, op=ALU.max, negate=True)
+
+        raw_factors = sb.tile([P, 2 * PAGES], F32, name="raw_factors")
+        nc.scalar.activation(out=raw_factors[:, 0:PAGES], in_=boost[:], func=ACT.Copy, scale=512.0)
+        th_sq = sb.tile([P, PAGES], F32, name="th_sq")
+        nc.scalar.activation(out=th_sq[:], in_=th[:], func=ACT.Square)
+        nc.scalar.activation(out=raw_factors[:, PAGES:], in_=th_sq[:], func=ACT.Identity, scale=consts[:, 3:4], bias=consts[:, 2:3])
+
+        vs = sb.tile([P, SLOTS], U8, name="vs", tag="boost_then_vs", align_bytes=64)
+
+        c0 = ps.tile([P, SLOTS], F32, name="c0")
+        for h, cols in enumerate(halves):
+            nc.vector.tensor_copy(vs[:, cols], v_bytes[:].indirect(list_halves[h]))
+            nc.tensor.matmul_mx(
+                out=c0[:, cols], lhsT=g_codes[:].bitcast(FP8X4), lhsT_scale=g_scales[:],
+                rhs=vw[h][:].bitcast(FP4X4), rhs_scale=vs[:, cols], start=True, stop=True,
+            )
+
+        p = sb.tile([P, SLOTS], F32, name="p")
+        z = sb.tile([P, 1], F32, name="z")
+        nc.scalar.activation(out=p[:], in_=s[:], func=ACT.Exp, bias=neg_max[:], accum_out=z[:])
+        inv_z = sb.tile([P, 1], F32, name="inv_z")
+        nc.vector.reciprocal(out=inv_z[:], in_=z[:])
+
+        weighted = sb.tile([P, SLOTS], F32, name="weighted")
+        mean_c0 = sb.tile([P, 1], F32, name="mean_c0")
+        nc.vector.scalar_tensor_tensor(
+            out=weighted[:], in0=p[:], scalar=inv_z[:], in1=c0[:], op0=ALU.mult, op1=ALU.mult, accum_out=mean_c0[:]
+        )
+        factors = sb.tile([P, 2 * PAGES], F32, name="factors")
+        nc.scalar.activation(out=factors[:], in_=raw_factors[:], func=ACT.Copy, scale=inv_z[:])
+
+        ds = sb.tile([P, SLOTS], F32, name="ds")
+        for cols in halves:
+            nc.vector.scalar_tensor_tensor(
+                out=ds[:, cols], in0=c0[:, cols], scalar=mean_c0[:], in1=p[:, cols], op0=ALU.subtract, op1=ALU.mult
+            )
+        direct = sb.tile([P, SLOTS], F32, name="direct")
+        for g in range(HPAGES):
+            cols = slice(g * PAGE, (g + 1) * PAGE)
+            nc.scalar.activation(out=direct[:, cols], in_=ds[:, cols], func=ACT.Copy, scale=factors[:, g : g + 1])
+        nc.gpsimd.tensor_tensor(
+            out=by_page(direct[:, halves[1]]), in0=by_page(ds[:, halves[1]]),
+            in1=over_page(factors[:, page_halves[1]], HPAGES), op=ALU.mult,
+        )
+        ds_a = sb.tile([P, SLOTS], F32, name="ds_a")
+        for h, cols in enumerate(halves):
+            nc.vector.tensor_tensor(out=ds_a[:, cols], in0=a[h][:], in1=ds[:, cols], op=ALU.mult)
+        page_grad = sb.tile([P, PAGES], F32, name="page_grad")
+        for cols, pages in zip(halves, page_halves):
+            nc.vector.tensor_reduce(out=page_grad[:, pages], in_=by_page(ds_a[:, cols]), axis=AX.X, op=ALU.add)
+        shared = sb.tile([P, SLOTS], F32, name="shared")
+        for cols, pages in zip(halves, page_halves):
+            nc.vector.tensor_tensor(
+                out=by_page(shared[:, cols]), in0=over_page(page_grad[:, pages], HPAGES),
+                in1=over_page(factors[:, PAGES + pages.start : PAGES + pages.stop], HPAGES), op=ALU.mult,
+            )
+
+        nc.vector.tensor_tensor(window[:].indirect(offsets[:]), direct[:], shared[:], ALU.add)
+
+        start = 0
+        for width in OUT_CHUNKS:
+            cols = slice(start, start + width)
+            nc.vector.tensor_tensor(out=result[:, cols], in0=result[:, cols], in1=window[:, cols], op=ALU.add)
+            nc.sync.dma_start(out=out[:, cols], in_=result[:, cols])
+            start = start + width

@@ -15,19 +15,26 @@ ACT = mybir.ActivationFunctionType
 AX = mybir.AxisListType
 
 P = 128
-D = 512
-T = 2048
+PACK = 4
+K = P * PACK
+TOKENS = 2048
 SLOTS = 512
 PAGE = 16
 PAGES = SLOTS // PAGE
 HALF = SLOTS // 2
-HPAGES = PAGES // 2
-OUT_CHUNKS = (256, 512, 512, 512, 256)
+HALF_PAGES = PAGES // 2
+BLOCKS = K // 32
+LIST_ROWS = 16
 
-FLOPS = 2 * 2 * D * P * SLOTS
+QUERY_ROWS_ON_SCALAR = 72
+STORE_WIDTH = TOKENS // 8
+
+FLOPS = 2 * 2 * K * P * SLOTS
 
 
-def tile_attend_bpagemates_s_kernel(tc, query, keys_words, keys_scales, helpf, gout, vals_words, vals_scales, old, offs, out):
+def tile_attend_bpagemates_s_kernel(
+    tc, query, keys_words, keys_scales, helpf, gout, vals_words, vals_scales, old, offs, out
+):
     nc = tc.nc
     with ExitStack() as ctx:
         sb = ctx.enter_context(tc.tile_pool(name="sb", bufs=1))
@@ -36,119 +43,131 @@ def tile_attend_bpagemates_s_kernel(tc, query, keys_words, keys_scales, helpf, g
         def by_page(ap):
             return ap.rearrange("p (g j) -> p g j", j=PAGE)
 
-        def over_page(ap, n):
-            return ap.unsqueeze(2).to_broadcast([P, n, PAGE])
+        def over_page(ap):
+            return ap.unsqueeze(2).to_broadcast([P, HALF_PAGES, PAGE])
 
-        offsets = sb.tile([P, SLOTS // 16], U16, name="offsets")
-        k_words = sb.tile([P, T], U16, name="k_words")
-        v_words = sb.tile([P, T], U16, name="v_words")
-        k_bytes = sb.tile([P, T], U8, name="k_bytes")
-        v_bytes = sb.tile([P, T], U8, name="v_bytes")
-        q_raw = sb.tile([P, 4, P], F32, name="q_raw")
-        g_raw = sb.tile([P, 4, P], F32, name="g_raw")
-        help_col = sb.tile([P, 1], F32, name="help_col")
-        result = sb.tile([P, T], F32, name="result")
-        window = sb.tile([P, T], F32, name="window")
+        def page_slots(page):
+            return slice(page * PAGE, (page + 1) * PAGE)
+
+        offsets = sb.tile([P, SLOTS // LIST_ROWS], U16, name="offsets")
+        k_words = sb.tile([P, TOKENS], U16, name="k_words")
+        k_bytes = sb.tile([P, TOKENS], U8, name="k_bytes", tag="k_bytes_then_g_codes", align_bytes=64)
+        v_bytes = sb.tile([P, TOKENS], U8, name="v_bytes")
+        q_raw = sb.tile([P, PACK, P], F32, name="q_raw")
+        g_raw = sb.tile([P, PACK, P], F32, name="g_raw")
+        help_col = sb.tile([P, 1], F32, name="help_col", tag="help_then_v_words_then_result")
+        window = sb.tile([P, TOKENS], F32, name="window")
+
+        slot_halves = [slice(h * HALF, (h + 1) * HALF) for h in range(2)]
+        page_halves = [slice(h * HALF_PAGES, (h + 1) * HALF_PAGES) for h in range(2)]
+        list_halves = [offsets[:, h * HALF // LIST_ROWS : (h + 1) * HALF // LIST_ROWS] for h in range(2)]
 
         nc.vector.memset(k_bytes[:].bitcast(I32), 0)
-        nc.vector.memset(v_bytes[:].bitcast(I32), 0)
         nc.vector.memset(window[:], 0.0)
+        nc.vector.memset(v_bytes[:].bitcast(I32), 0)
 
-        def load_scale_rows(engine, tile, src):
-            for quad in range(4):
-                engine.dma_start(
-                    out=tile[32 * quad : 32 * quad + 4, :].bitcast(I32),
-                    in_=src[0, 4 * quad : 4 * quad + 4, :].bitcast(I32),
-                )
+        def load_scale_rows(tile, scales):
+            for r in range(4):
+                nc.sync.dma_start(out=tile[r:P:32, :].bitcast(I32), in_=scales[0, r:BLOCKS:4, :].bitcast(I32))
 
         nc.sync.dma_start(offsets[:], offs)
         nc.sync.dma_start(out=k_words[:].bitcast(I32), in_=keys_words[0].bitcast(I32))
-        load_scale_rows(nc.scalar, k_bytes, keys_scales)
-        nc.sync.dma_start(out=q_raw[:], in_=query.rearrange("(p j) w -> p j w", j=4))
-        nc.sync.dma_start(out=v_words[:].bitcast(I32), in_=vals_words[0].bitcast(I32))
-        nc.sync.dma_start(out=help_col[:], in_=helpf)
-        nc.sync.dma_start(out=g_raw[:], in_=gout.rearrange("(p j) w -> p j w", j=4))
-        load_scale_rows(nc.sync, v_bytes, vals_scales)
-        nc.sync.dma_start(out=result[:], in_=old)
+        nc.scalar.dma_start(out=help_col[:], in_=helpf)
+        nc.sync.dma_start(out=q_raw[:], in_=query.rearrange("(p j) w -> p j w", j=PACK))
+        nc.sync.dma_start(out=g_raw[:], in_=gout.rearrange("(p j) w -> p j w", j=PACK))
+        load_scale_rows(k_bytes, keys_scales)
 
-        def round_and_interleave(raw, name):
-            grouped = sb.tile([P, P, 4], BF16, name=name, align_bytes=64)
-            nc.scalar.activation(out=grouped[:], in_=raw[:].rearrange("p j w -> p w j"), func=ACT.Copy)
-            return grouped
+        row_consts = sb.tile([P, 4], F32, name="row_consts")
+        boost_bias, boost_scale, slope_bias, slope_scale = [row_consts[:, c : c + 1] for c in range(4)]
+        nc.scalar.activation(out=boost_bias, in_=help_col[:], func=ACT.Identity, scale=0.5, bias=1.0)
+        nc.scalar.activation(out=boost_scale, in_=help_col[:], func=ACT.Copy, scale=0.5)
+        nc.scalar.activation(out=slope_bias, in_=help_col[:], func=ACT.Copy, scale=32.0)
+        nc.scalar.activation(out=slope_scale, in_=help_col[:], func=ACT.Copy, scale=-32.0)
 
-        def quantise(grouped, name):
-            codes = sb.tile([P, P], U32, name=name + "_codes", align_bytes=64)
+        v_words = sb.tile([P, TOKENS], U16, name="v_words", tag="help_then_v_words_then_result")
+        nc.scalar.dma_start(out=v_words[:].bitcast(I32), in_=vals_words[0].bitcast(I32))
+        load_scale_rows(v_bytes, vals_scales)
+
+        q_bf = sb.tile([P, P, PACK], BF16, name="q_bf", align_bytes=64)
+        q_by_row = q_raw[:].rearrange("p j w -> p w j")
+        nc.scalar.activation(
+            out=q_bf[:, 0:QUERY_ROWS_ON_SCALAR, :], in_=q_by_row[:, 0:QUERY_ROWS_ON_SCALAR, :], func=ACT.Copy
+        )
+        nc.gpsimd.tensor_copy(out=q_bf[:, QUERY_ROWS_ON_SCALAR:P, :], in_=q_by_row[:, QUERY_ROWS_ON_SCALAR:P, :])
+        g_bf = sb.tile([P, P, PACK], BF16, name="g_bf", align_bytes=64)
+        nc.scalar.activation(out=g_bf[:], in_=g_raw[:].rearrange("p j w -> p w j"), func=ACT.Copy)
+
+        def quantise(rounded, name, codes_tag):
+            codes = sb.tile([P, P], U32, name=name + "_codes", tag=codes_tag, align_bytes=64)
             scales = sb.tile([P, P], U8, name=name + "_scales", align_bytes=64)
-            nc.vector.quantize_mx(out=codes[:].bitcast(FP8X4), scales=scales[:], in_=grouped[:].rearrange("p w j -> p (w j)"))
+            nc.vector.quantize_mx(
+                out=codes[:].bitcast(FP8X4), scales=scales[:], in_=rounded[:].rearrange("p w j -> p (w j)")
+            )
             return codes, scales
 
-        q_bf = round_and_interleave(q_raw, "q_bf")
-        consts = sb.tile([P, 4], F32, name="consts")
-        nc.scalar.activation(out=consts[:, 0:1], in_=help_col[:], func=ACT.Identity, scale=0.5, bias=1.0)
-        nc.scalar.activation(out=consts[:, 1:2], in_=help_col[:], func=ACT.Copy, scale=0.5)
-        nc.scalar.activation(out=consts[:, 2:3], in_=help_col[:], func=ACT.Copy, scale=32.0)
-        nc.scalar.activation(out=consts[:, 3:4], in_=help_col[:], func=ACT.Copy, scale=-32.0)
-        g_bf = round_and_interleave(g_raw, "g_bf")
-
-        halves = [slice(h * HALF, (h + 1) * HALF) for h in range(2)]
-        page_halves = [slice(h * HPAGES, (h + 1) * HPAGES) for h in range(2)]
-        list_halves = [offsets[:, h * HALF // 16 : (h + 1) * HALF // 16] for h in range(2)]
-
+        kw = sb.tile([P, SLOTS], U16, name="kw", align_bytes=64)
+        nc.vector.tensor_copy(kw[:], k_words[:].indirect(offsets[:]))
+        q_codes, q_scales = quantise(q_bf, "q", "q_codes")
         a = []
         for h in range(2):
             ks = sb.tile([P, HALF], U8, name="ks%d" % h, tag="ks_then_vw%d" % h, align_bytes=64)
             nc.vector.tensor_copy(ks[:], k_bytes[:].indirect(list_halves[h]))
-            kw = sb.tile([P, HALF], U16, name="kw%d" % h, align_bytes=64)
-            nc.vector.tensor_copy(kw[:], k_words[:].indirect(list_halves[h]))
-            if h == 0:
-                q_codes, q_scales = quantise(q_bf, "q")
             bank = ps.tile([P, HALF], F32, name="a%d" % h)
             nc.tensor.matmul_mx(
                 out=bank[:], lhsT=q_codes[:].bitcast(FP8X4), lhsT_scale=q_scales[:],
-                rhs=kw[:].bitcast(FP4X4), rhs_scale=ks[:], start=True, stop=True,
+                rhs=kw[:, slot_halves[h]].bitcast(FP4X4), rhs_scale=ks[:], start=True, stop=True,
             )
             a.append(bank)
+        g_codes, g_scales = quantise(g_bf, "g", "k_bytes_then_g_codes")
 
         page_sum = sb.tile([P, PAGES], F32, name="page_sum")
-        th = sb.tile([P, PAGES], F32, name="th")
-        boost = sb.tile([P, PAGES], F32, name="boost", tag="boost_then_vs", align_bytes=64)
-        for h in range(2):
-            nc.vector.tensor_reduce(out=page_sum[:, page_halves[h]], in_=by_page(a[h][:]), axis=AX.X, op=ALU.add)
-        for pages in page_halves:
-            nc.scalar.activation(out=th[:, pages], in_=page_sum[:, pages], func=ACT.Tanh, scale=0.125)
-        for pages in page_halves:
-            nc.scalar.activation(out=boost[:, pages], in_=th[:, pages], func=ACT.Identity, scale=consts[:, 1:2], bias=consts[:, 0:1])
-
+        th = sb.tile([P, PAGES], F32, name="th", tag="th_then_vs0", align_bytes=64)
         vw = []
         for h in range(2):
+            nc.vector.tensor_reduce(out=page_sum[:, page_halves[h]], in_=by_page(a[h][:]), axis=AX.X, op=ALU.add)
             words = sb.tile([P, HALF], U16, name="vw%d" % h, tag="ks_then_vw%d" % h, align_bytes=64)
             nc.vector.tensor_copy(words[:], v_words[:].indirect(list_halves[h]))
             vw.append(words)
-        g_codes, g_scales = quantise(g_bf, "g")
+        result = sb.tile([P, TOKENS], F32, name="result", tag="help_then_v_words_then_result")
+        nc.sync.dma_start(out=result[:], in_=old)
+
+        for pages in page_halves:
+            nc.scalar.activation(out=th[:, pages], in_=page_sum[:, pages], func=ACT.Tanh, scale=0.125)
+        boost = []
+        for h, tag in enumerate(("boost0", "boost1_then_slope")):
+            half_boost = sb.tile([P, HALF_PAGES], F32, name="boost%d" % h, tag=tag)
+            nc.scalar.activation(
+                out=half_boost[:], in_=th[:, page_halves[h]], func=ACT.Identity, scale=boost_scale, bias=boost_bias
+            )
+            boost.append(half_boost)
+        th_sq = sb.tile([P, PAGES], F32, name="th_sq", tag="th_sq_then_vs1", align_bytes=64)
+        nc.scalar.activation(out=th_sq[:], in_=th[:], func=ACT.Square)
+        boost_512 = sb.tile([P, PAGES], F32, name="boost_512")
+        for h in range(2):
+            nc.scalar.activation(out=boost_512[:, page_halves[h]], in_=boost[h][:], func=ACT.Copy, scale=512.0)
 
         s = sb.tile([P, SLOTS], F32, name="s")
         for h in range(2):
             nc.vector.tensor_tensor(
-                out=by_page(s[:, halves[h]]), in0=by_page(a[h][:]), in1=over_page(boost[:, page_halves[h]], HPAGES), op=ALU.mult
+                out=by_page(s[:, slot_halves[h]]), in0=by_page(a[h][:]), in1=over_page(boost[h][:]), op=ALU.mult
             )
-        neg_max = sb.tile([P, 1], F32, name="neg_max")
-        nc.vector.tensor_reduce(out=neg_max[:], in_=s[:], axis=AX.X, op=ALU.max, negate=True)
-
-        raw_factors = sb.tile([P, 2 * PAGES], F32, name="raw_factors")
-        nc.scalar.activation(out=raw_factors[:, 0:PAGES], in_=boost[:], func=ACT.Copy, scale=512.0)
-        th_sq = sb.tile([P, PAGES], F32, name="th_sq")
-        nc.scalar.activation(out=th_sq[:], in_=th[:], func=ACT.Square)
-        nc.scalar.activation(out=raw_factors[:, PAGES:], in_=th_sq[:], func=ACT.Identity, scale=consts[:, 3:4], bias=consts[:, 2:3])
-
-        vs = sb.tile([P, SLOTS], U8, name="vs", tag="boost_then_vs", align_bytes=64)
 
         c0 = ps.tile([P, SLOTS], F32, name="c0")
-        for h, cols in enumerate(halves):
-            nc.vector.tensor_copy(vs[:, cols], v_bytes[:].indirect(list_halves[h]))
+
+        def value_product(h, scales_tag):
+            vs = sb.tile([P, HALF], U8, name="vs%d" % h, tag=scales_tag, align_bytes=64)
+            nc.vector.tensor_copy(vs[:], v_bytes[:].indirect(list_halves[h]))
             nc.tensor.matmul_mx(
-                out=c0[:, cols], lhsT=g_codes[:].bitcast(FP8X4), lhsT_scale=g_scales[:],
-                rhs=vw[h][:].bitcast(FP4X4), rhs_scale=vs[:, cols], start=True, stop=True,
+                out=c0[:, slot_halves[h]], lhsT=g_codes[:].bitcast(FP8X4), lhsT_scale=g_scales[:],
+                rhs=vw[h][:].bitcast(FP4X4), rhs_scale=vs[:], start=True, stop=True,
             )
+
+        value_product(0, "th_then_vs0")
+        neg_max = sb.tile([P, 1], F32, name="neg_max")
+        nc.vector.tensor_reduce(out=neg_max[:], in_=s[:], axis=AX.X, op=ALU.max, negate=True)
+        slope = sb.tile([P, PAGES], F32, name="slope", tag="boost1_then_slope")
+        nc.scalar.activation(out=slope[:], in_=th_sq[:], func=ACT.Identity, scale=slope_scale, bias=slope_bias)
+        value_product(1, "th_sq_then_vs1")
 
         p = sb.tile([P, SLOTS], F32, name="p")
         z = sb.tile([P, 1], F32, name="z")
@@ -156,45 +175,54 @@ def tile_attend_bpagemates_s_kernel(tc, query, keys_words, keys_scales, helpf, g
         inv_z = sb.tile([P, 1], F32, name="inv_z")
         nc.vector.reciprocal(out=inv_z[:], in_=z[:])
 
-        weighted = sb.tile([P, SLOTS], F32, name="weighted")
+        a_slope = sb.tile([P, SLOTS], F32, name="a_slope")
+        for h in range(2):
+            nc.vector.tensor_tensor(
+                out=by_page(a_slope[:, slot_halves[h]]), in0=by_page(a[h][:]),
+                in1=over_page(slope[:, page_halves[h]]), op=ALU.mult,
+            )
+
+        mean_terms = sb.tile([P, SLOTS], F32, name="mean_terms")
         mean_c0 = sb.tile([P, 1], F32, name="mean_c0")
         nc.vector.scalar_tensor_tensor(
-            out=weighted[:], in0=p[:], scalar=inv_z[:], in1=c0[:], op0=ALU.mult, op1=ALU.mult, accum_out=mean_c0[:]
+            out=mean_terms[:], in0=p[:], scalar=inv_z[:], in1=c0[:], op0=ALU.mult, op1=ALU.mult, accum_out=mean_c0[:]
         )
-        factors = sb.tile([P, 2 * PAGES], F32, name="factors")
-        nc.scalar.activation(out=factors[:], in_=raw_factors[:], func=ACT.Copy, scale=inv_z[:])
+        page_factor = sb.tile([P, PAGES], F32, name="page_factor")
+        nc.scalar.activation(out=page_factor[:], in_=boost_512[:], func=ACT.Copy, scale=inv_z[:])
 
-        ds = sb.tile([P, SLOTS], F32, name="ds")
-        for cols in halves:
+        centred = sb.tile([P, SLOTS], F32, name="centred")
+        for cols in slot_halves:
             nc.vector.scalar_tensor_tensor(
-                out=ds[:, cols], in0=c0[:, cols], scalar=mean_c0[:], in1=p[:, cols], op0=ALU.subtract, op1=ALU.mult
+                out=centred[:, cols], in0=c0[:, cols], scalar=mean_c0[:], in1=p[:, cols],
+                op0=ALU.subtract, op1=ALU.mult,
             )
-        direct = sb.tile([P, SLOTS], F32, name="direct")
-        for g in range(HPAGES):
-            cols = slice(g * PAGE, (g + 1) * PAGE)
-            nc.scalar.activation(out=direct[:, cols], in_=ds[:, cols], func=ACT.Copy, scale=factors[:, g : g + 1])
-        nc.gpsimd.tensor_tensor(
-            out=by_page(direct[:, halves[1]]), in0=by_page(ds[:, halves[1]]),
-            in1=over_page(factors[:, page_halves[1]], HPAGES), op=ALU.mult,
-        )
-        ds_a = sb.tile([P, SLOTS], F32, name="ds_a")
-        for h, cols in enumerate(halves):
-            nc.vector.tensor_tensor(out=ds_a[:, cols], in0=a[h][:], in1=ds[:, cols], op=ALU.mult)
-        page_grad = sb.tile([P, PAGES], F32, name="page_grad")
-        for cols, pages in zip(halves, page_halves):
-            nc.vector.tensor_reduce(out=page_grad[:, pages], in_=by_page(ds_a[:, cols]), axis=AX.X, op=ALU.add)
-        shared = sb.tile([P, SLOTS], F32, name="shared")
-        for cols, pages in zip(halves, page_halves):
-            nc.vector.tensor_tensor(
-                out=by_page(shared[:, cols]), in0=over_page(page_grad[:, pages], HPAGES),
-                in1=over_page(factors[:, PAGES + pages.start : PAGES + pages.stop], HPAGES), op=ALU.mult,
+        first_direct = sb.tile([P, HALF], F32, name="first_direct")
+        for page in range(HALF_PAGES):
+            nc.scalar.activation(
+                out=first_direct[:, page_slots(page)], in_=centred[:, page_slots(page)], func=ACT.Copy,
+                scale=page_factor[:, page : page + 1],
             )
+        gate_terms = sb.tile([P, SLOTS], F32, name="gate_terms")
+        for cols in slot_halves:
+            nc.vector.scalar_tensor_tensor(
+                out=gate_terms[:, cols], in0=centred[:, cols], scalar=inv_z[:], in1=a_slope[:, cols],
+                op0=ALU.mult, op1=ALU.mult,
+            )
+        page_term = sb.tile([P, PAGES], F32, name="page_term")
+        for cols, pages in zip(slot_halves, page_halves):
+            nc.vector.tensor_reduce(out=page_term[:, pages], in_=by_page(gate_terms[:, cols]), axis=AX.X, op=ALU.add)
+        first_shared = sb.tile([P, HALF], F32, name="first_shared")
+        nc.vector.tensor_copy(out=by_page(first_shared[:]), in_=over_page(page_term[:, page_halves[0]]))
+        nc.vector.tensor_tensor(window[:].indirect(list_halves[0]), first_direct[:], first_shared[:], ALU.add)
+        second_gs = sb.tile([P, HALF], F32, name="second_gs")
+        for page in range(HALF_PAGES, PAGES):
+            nc.scalar.activation(
+                out=second_gs[:, page_slots(page - HALF_PAGES)], in_=centred[:, page_slots(page)], func=ACT.Identity,
+                scale=page_factor[:, page : page + 1], bias=page_term[:, page : page + 1],
+            )
+        nc.vector.tensor_copy(window[:].indirect(list_halves[1]), second_gs[:])
 
-        nc.vector.tensor_tensor(window[:].indirect(offsets[:]), direct[:], shared[:], ALU.add)
-
-        start = 0
-        for width in OUT_CHUNKS:
-            cols = slice(start, start + width)
+        for first_col in range(0, TOKENS, STORE_WIDTH):
+            cols = slice(first_col, first_col + STORE_WIDTH)
             nc.vector.tensor_tensor(out=result[:, cols], in0=result[:, cols], in1=window[:, cols], op=ALU.add)
             nc.sync.dma_start(out=out[:, cols], in_=result[:, cols])
-            start = start + width

from contextlib import ExitStack

import concourse.mybir as mybir

F32 = mybir.dt.float32
BF16 = mybir.dt.bfloat16
I32 = mybir.dt.int32
U32 = mybir.dt.uint32
U16 = mybir.dt.uint16
U8 = mybir.dt.uint8
FP8X4 = mybir.dt.float8_e4m3fn_x4
FP4X4 = mybir.dt.float4_e2m1fn_x4
ALU = mybir.AluOpType
ACT = mybir.ActivationFunctionType
AX = mybir.AxisListType

P = 128
PACK = 4
K = P * PACK
TOKENS = 2048
SLOTS = 512
PAGE = 16
PAGES = SLOTS // PAGE
HALF = SLOTS // 2
HALF_PAGES = PAGES // 2
BLOCKS = K // 32
LIST_ROWS = 16

QUERY_ROWS_ON_SCALAR = 72
STORE_WIDTH = TOKENS // 8

FLOPS = 2 * 2 * K * P * SLOTS


def tile_attend_bpagemates_s_kernel(
    tc, query, keys_words, keys_scales, helpf, gout, vals_words, vals_scales, old, offs, out
):
    nc = tc.nc
    with ExitStack() as ctx:
        sb = ctx.enter_context(tc.tile_pool(name="sb", bufs=1))
        ps = ctx.enter_context(tc.psum_pool(name="ps", bufs=1))

        def by_page(ap):
            return ap.rearrange("p (g j) -> p g j", j=PAGE)

        def over_page(ap):
            return ap.unsqueeze(2).to_broadcast([P, HALF_PAGES, PAGE])

        def page_slots(page):
            return slice(page * PAGE, (page + 1) * PAGE)

        offsets = sb.tile([P, SLOTS // LIST_ROWS], U16, name="offsets")
        k_words = sb.tile([P, TOKENS], U16, name="k_words")
        k_bytes = sb.tile([P, TOKENS], U8, name="k_bytes", tag="k_bytes_then_g_codes", align_bytes=64)
        v_bytes = sb.tile([P, TOKENS], U8, name="v_bytes")
        q_raw = sb.tile([P, PACK, P], F32, name="q_raw")
        g_raw = sb.tile([P, PACK, P], F32, name="g_raw")
        help_col = sb.tile([P, 1], F32, name="help_col", tag="help_then_v_words_then_result")
        window = sb.tile([P, TOKENS], F32, name="window")

        slot_halves = [slice(h * HALF, (h + 1) * HALF) for h in range(2)]
        page_halves = [slice(h * HALF_PAGES, (h + 1) * HALF_PAGES) for h in range(2)]
        list_halves = [offsets[:, h * HALF // LIST_ROWS : (h + 1) * HALF // LIST_ROWS] for h in range(2)]

        nc.vector.memset(k_bytes[:].bitcast(I32), 0)
        nc.vector.memset(window[:], 0.0)
        nc.vector.memset(v_bytes[:].bitcast(I32), 0)

        def load_scale_rows(tile, scales):
            for r in range(4):
                nc.sync.dma_start(out=tile[r:P:32, :].bitcast(I32), in_=scales[0, r:BLOCKS:4, :].bitcast(I32))

        nc.sync.dma_start(offsets[:], offs)
        nc.sync.dma_start(out=k_words[:].bitcast(I32), in_=keys_words[0].bitcast(I32))
        nc.scalar.dma_start(out=help_col[:], in_=helpf)
        nc.sync.dma_start(out=q_raw[:], in_=query.rearrange("(p j) w -> p j w", j=PACK))
        nc.sync.dma_start(out=g_raw[:], in_=gout.rearrange("(p j) w -> p j w", j=PACK))
        load_scale_rows(k_bytes, keys_scales)

        row_consts = sb.tile([P, 4], F32, name="row_consts")
        boost_bias, boost_scale, slope_bias, slope_scale = [row_consts[:, c : c + 1] for c in range(4)]
        nc.scalar.activation(out=boost_bias, in_=help_col[:], func=ACT.Identity, scale=0.5, bias=1.0)
        nc.scalar.activation(out=boost_scale, in_=help_col[:], func=ACT.Copy, scale=0.5)
        nc.scalar.activation(out=slope_bias, in_=help_col[:], func=ACT.Copy, scale=32.0)
        nc.scalar.activation(out=slope_scale, in_=help_col[:], func=ACT.Copy, scale=-32.0)

        v_words = sb.tile([P, TOKENS], U16, name="v_words", tag="help_then_v_words_then_result")
        nc.scalar.dma_start(out=v_words[:].bitcast(I32), in_=vals_words[0].bitcast(I32))
        load_scale_rows(v_bytes, vals_scales)

        q_bf = sb.tile([P, P, PACK], BF16, name="q_bf", align_bytes=64)
        q_by_row = q_raw[:].rearrange("p j w -> p w j")
        nc.scalar.activation(
            out=q_bf[:, 0:QUERY_ROWS_ON_SCALAR, :], in_=q_by_row[:, 0:QUERY_ROWS_ON_SCALAR, :], func=ACT.Copy
        )
        nc.gpsimd.tensor_copy(out=q_bf[:, QUERY_ROWS_ON_SCALAR:P, :], in_=q_by_row[:, QUERY_ROWS_ON_SCALAR:P, :])
        g_bf = sb.tile([P, P, PACK], BF16, name="g_bf", align_bytes=64)
        nc.scalar.activation(out=g_bf[:], in_=g_raw[:].rearrange("p j w -> p w j"), func=ACT.Copy)

        def quantise(rounded, name, codes_tag):
            codes = sb.tile([P, P], U32, name=name + "_codes", tag=codes_tag, align_bytes=64)
            scales = sb.tile([P, P], U8, name=name + "_scales", align_bytes=64)
            nc.vector.quantize_mx(
                out=codes[:].bitcast(FP8X4), scales=scales[:], in_=rounded[:].rearrange("p w j -> p (w j)")
            )
            return codes, scales

        kw = sb.tile([P, SLOTS], U16, name="kw", align_bytes=64)
        nc.vector.tensor_copy(kw[:], k_words[:].indirect(offsets[:]))
        q_codes, q_scales = quantise(q_bf, "q", "q_codes")
        a = []
        for h in range(2):
            ks = sb.tile([P, HALF], U8, name="ks%d" % h, tag="ks_then_vw%d" % h, align_bytes=64)
            nc.vector.tensor_copy(ks[:], k_bytes[:].indirect(list_halves[h]))
            bank = ps.tile([P, HALF], F32, name="a%d" % h)
            nc.tensor.matmul_mx(
                out=bank[:], lhsT=q_codes[:].bitcast(FP8X4), lhsT_scale=q_scales[:],
                rhs=kw[:, slot_halves[h]].bitcast(FP4X4), rhs_scale=ks[:], start=True, stop=True,
            )
            a.append(bank)
        g_codes, g_scales = quantise(g_bf, "g", "k_bytes_then_g_codes")

        page_sum = sb.tile([P, PAGES], F32, name="page_sum")
        th = sb.tile([P, PAGES], F32, name="th", tag="th_then_vs0", align_bytes=64)
        vw = []
        for h in range(2):
            nc.vector.tensor_reduce(out=page_sum[:, page_halves[h]], in_=by_page(a[h][:]), axis=AX.X, op=ALU.add)
            words = sb.tile([P, HALF], U16, name="vw%d" % h, tag="ks_then_vw%d" % h, align_bytes=64)
            nc.vector.tensor_copy(words[:], v_words[:].indirect(list_halves[h]))
            vw.append(words)
        result = sb.tile([P, TOKENS], F32, name="result", tag="help_then_v_words_then_result")
        nc.sync.dma_start(out=result[:], in_=old)

        for pages in page_halves:
            nc.scalar.activation(out=th[:, pages], in_=page_sum[:, pages], func=ACT.Tanh, scale=0.125)
        boost = []
        for h, tag in enumerate(("boost0", "boost1_then_slope")):
            half_boost = sb.tile([P, HALF_PAGES], F32, name="boost%d" % h, tag=tag)
            nc.scalar.activation(
                out=half_boost[:], in_=th[:, page_halves[h]], func=ACT.Identity, scale=boost_scale, bias=boost_bias
            )
            boost.append(half_boost)
        th_sq = sb.tile([P, PAGES], F32, name="th_sq", tag="th_sq_then_vs1", align_bytes=64)
        nc.scalar.activation(out=th_sq[:], in_=th[:], func=ACT.Square)
        boost_512 = sb.tile([P, PAGES], F32, name="boost_512")
        for h in range(2):
            nc.scalar.activation(out=boost_512[:, page_halves[h]], in_=boost[h][:], func=ACT.Copy, scale=512.0)

        s = sb.tile([P, SLOTS], F32, name="s")
        for h in range(2):
            nc.vector.tensor_tensor(
                out=by_page(s[:, slot_halves[h]]), in0=by_page(a[h][:]), in1=over_page(boost[h][:]), op=ALU.mult
            )

        c0 = ps.tile([P, SLOTS], F32, name="c0")

        def value_product(h, scales_tag):
            vs = sb.tile([P, HALF], U8, name="vs%d" % h, tag=scales_tag, align_bytes=64)
            nc.vector.tensor_copy(vs[:], v_bytes[:].indirect(list_halves[h]))
            nc.tensor.matmul_mx(
                out=c0[:, slot_halves[h]], lhsT=g_codes[:].bitcast(FP8X4), lhsT_scale=g_scales[:],
                rhs=vw[h][:].bitcast(FP4X4), rhs_scale=vs[:], start=True, stop=True,
            )

        value_product(0, "th_then_vs0")
        neg_max = sb.tile([P, 1], F32, name="neg_max")
        nc.vector.tensor_reduce(out=neg_max[:], in_=s[:], axis=AX.X, op=ALU.max, negate=True)
        slope = sb.tile([P, PAGES], F32, name="slope", tag="boost1_then_slope")
        nc.scalar.activation(out=slope[:], in_=th_sq[:], func=ACT.Identity, scale=slope_scale, bias=slope_bias)
        value_product(1, "th_sq_then_vs1")

        p = sb.tile([P, SLOTS], F32, name="p")
        z = sb.tile([P, 1], F32, name="z")
        nc.scalar.activation(out=p[:], in_=s[:], func=ACT.Exp, bias=neg_max[:], accum_out=z[:])
        inv_z = sb.tile([P, 1], F32, name="inv_z")
        nc.vector.reciprocal(out=inv_z[:], in_=z[:])

        a_slope = sb.tile([P, SLOTS], F32, name="a_slope")
        for h in range(2):
            nc.vector.tensor_tensor(
                out=by_page(a_slope[:, slot_halves[h]]), in0=by_page(a[h][:]),
                in1=over_page(slope[:, page_halves[h]]), op=ALU.mult,
            )

        mean_terms = sb.tile([P, SLOTS], F32, name="mean_terms")
        mean_c0 = sb.tile([P, 1], F32, name="mean_c0")
        nc.vector.scalar_tensor_tensor(
            out=mean_terms[:], in0=p[:], scalar=inv_z[:], in1=c0[:], op0=ALU.mult, op1=ALU.mult, accum_out=mean_c0[:]
        )
        page_factor = sb.tile([P, PAGES], F32, name="page_factor")
        nc.scalar.activation(out=page_factor[:], in_=boost_512[:], func=ACT.Copy, scale=inv_z[:])

        centred = sb.tile([P, SLOTS], F32, name="centred")
        for cols in slot_halves:
            nc.vector.scalar_tensor_tensor(
                out=centred[:, cols], in0=c0[:, cols], scalar=mean_c0[:], in1=p[:, cols],
                op0=ALU.subtract, op1=ALU.mult,
            )
        first_direct = sb.tile([P, HALF], F32, name="first_direct")
        for page in range(HALF_PAGES):
            nc.scalar.activation(
                out=first_direct[:, page_slots(page)], in_=centred[:, page_slots(page)], func=ACT.Copy,
                scale=page_factor[:, page : page + 1],
            )
        gate_terms = sb.tile([P, SLOTS], F32, name="gate_terms")
        for cols in slot_halves:
            nc.vector.scalar_tensor_tensor(
                out=gate_terms[:, cols], in0=centred[:, cols], scalar=inv_z[:], in1=a_slope[:, cols],
                op0=ALU.mult, op1=ALU.mult,
            )
        page_term = sb.tile([P, PAGES], F32, name="page_term")
        for cols, pages in zip(slot_halves, page_halves):
            nc.vector.tensor_reduce(out=page_term[:, pages], in_=by_page(gate_terms[:, cols]), axis=AX.X, op=ALU.add)
        first_shared = sb.tile([P, HALF], F32, name="first_shared")
        nc.vector.tensor_copy(out=by_page(first_shared[:]), in_=over_page(page_term[:, page_halves[0]]))
        nc.vector.tensor_tensor(window[:].indirect(list_halves[0]), first_direct[:], first_shared[:], ALU.add)
        second_gs = sb.tile([P, HALF], F32, name="second_gs")
        for page in range(HALF_PAGES, PAGES):
            nc.scalar.activation(
                out=second_gs[:, page_slots(page - HALF_PAGES)], in_=centred[:, page_slots(page)], func=ACT.Identity,
                scale=page_factor[:, page : page + 1], bias=page_term[:, page : page + 1],
            )
        nc.vector.tensor_copy(window[:].indirect(list_halves[1]), second_gs[:])

        for first_col in range(0, TOKENS, STORE_WIDTH):
            cols = slice(first_col, first_col + STORE_WIDTH)
            nc.vector.tensor_tensor(out=result[:, cols], in0=result[:, cols], in1=window[:, cols], op=ALU.add)
            nc.sync.dma_start(out=out[:, cols], in_=result[:, cols])
